import numpy as np
import ml_dtypes


def mxq(x, axis, fmt="e4m3"):
    dtype, down = {"e4m3": (ml_dtypes.float8_e4m3fn, 7), "e5m2": (ml_dtypes.float8_e5m2, 14)}[fmt]
    v = np.moveaxis(np.asarray(x, np.float32).astype(ml_dtypes.bfloat16).astype(np.float64), axis, -1)
    blocks = v.reshape(v.shape[:-1] + (-1, 32))
    amax = np.abs(blocks).max(-1, keepdims=True)
    byte = np.maximum(np.where(amax > 0, np.frexp(amax)[1] - 1 + 127, 0) - down, 1)
    scale = np.exp2(byte - 127.0)
    codes = (blocks / scale).astype(np.float32).astype(dtype).astype(np.float64)
    return np.moveaxis((codes * scale).reshape(v.shape), -1, axis)


WIDE = False


def mx_kscale(k):
    if not WIDE:
        return np.ones(k)
    levels = np.array([10, -10, 5, -5, 0])
    if k % 512:
        return np.exp2(np.random.permutation(np.resize(levels, k // 32))).repeat(32)
    a = np.empty((k // 512, 16))
    for p in range(k // 512):
        a[p, :8] = np.random.permutation(np.resize(levels, 8))
        for g in range(8):
            far = levels[np.abs(levels - a[p, g]) >= 10]
            a[p, g + 8] = far[np.random.randint(len(far))]
    return np.exp2(a.ravel()).repeat(32)


def f64(x):
    return np.asarray(x).astype(np.float64)


def striped(idx):
    return np.tile(np.asarray(idx).reshape(-1, 16).T, (8, 1)).astype(np.uint16)


def unstriped(offs):
    return offs[:16].T.reshape(-1).astype(np.int64)


E2M1 = np.array([0.0, 0.5, 1.0, 1.5, 2.0, 3.0, 4.0, 6.0, -0.0, -0.5, -1.0, -1.5, -2.0, -3.0, -4.0, -6.0])


def pack_weight(w, fmt):
    k, n = w.shape
    w = f64(np.asarray(w, np.float32).astype(ml_dtypes.bfloat16)).reshape(k // 32, 32, n)
    amax = np.abs(w).max(1)
    if fmt == "e4m3":
        byte = np.frexp(amax)[1] - 1 + 127 - 7
    else:
        mant, ex = np.frexp(amax / 6.0)
        byte = np.where(mant > 0.5, ex, ex - 1) + 127
    byte = np.clip(np.where(amax > 0, byte, 1), 1, 254)
    scaled = (w * np.exp2(127.0 - byte)[:, None, :]).reshape(k, n).astype(np.float32)
    by_word = np.ascontiguousarray(scaled.reshape(k // 512, 128, 4, n).transpose(0, 1, 3, 2))
    if fmt == "e4m3":
        words = by_word.astype(ml_dtypes.float8_e4m3fn).view(np.uint8)
    else:
        c = by_word.astype(ml_dtypes.float4_e2m1fn).view(np.uint8) & 0xF
        words = (c[..., 0::2] | (c[..., 1::2] << 4)).reshape(k // 512, 128, 2 * n)
    return np.ascontiguousarray(words), np.ascontiguousarray(byte.astype(np.uint8).reshape(k // 512, 16, n))


def unpack_weight(words, scales, fmt):
    g, _, n = scales.shape
    words = np.ascontiguousarray(words).reshape(g, 128, n, -1)
    if fmt == "e4m3":
        vals = words.view(ml_dtypes.float8_e4m3fn).astype(np.float64)
    else:
        nib = np.empty((g, 128, n, 4), np.uint8)
        nib[..., 0::2] = words & 0xF
        nib[..., 1::2] = words >> 4
        vals = E2M1[nib]
    vals = vals * np.repeat(np.exp2(scales.astype(np.float64) - 127.0), 8, axis=1)[..., None]
    return vals.transpose(0, 1, 3, 2).reshape(g * 512, n)


def sigmoid(v):
    return 1.0 / (1.0 + np.exp(-v))


D, T, I, Q, E, U, K = 512, 2048, 512, 128, 512, 1024, 16


def setup_inputs():
    n = np.random.standard_normal
    idx = np.random.permutation(T)[:I]
    idx2 = np.random.permutation(U)[:I]
    fd = mx_kscale(D)
    fi = mx_kscale(I)
    ti = np.ones(T)
    ti[idx] = fi
    keysp = pack_weight(n((D, T)) / fd[:, None], "e2m1")
    return {
        "query": (n((D, Q)) * 1.2 / np.sqrt(D) * fd[:, None]).astype(np.float32),
        "query2": (n((D, Q)) * 1.5 / np.sqrt(D) * fd[:, None]).astype(np.float32),
        "keys_words": keysp[0],
        "keys_scales": keysp[1],
        "notes": (n((D, U)) / fd[:, None]).astype(np.float32),
        "lam": (np.random.uniform(-0.8, 0.8, (Q, 1))).astype(np.float32),
        "os": (np.random.uniform(4.0, 16.0, (1, I)) * fi).astype(np.float32),
        "vals": (n((E, T)) / ti).astype(np.float32),
        "target": (n((Q, E))).astype(np.float32),
        "offs": striped(idx),
        "offs2": striped(idx2),
    }


def reference(query, query2, keys_words, keys_scales, notes, lam, os, vals, target, offs, offs2):
    idx = unstriped(offs)
    idx2 = unstriped(offs2)
    keysu = unpack_weight(keys_words, keys_scales, "e2m1")
    queryq = mxq(f64(query), 0, "e4m3")
    keysidxg = keysu[:, idx]
    a = queryq.T @ keysidxg
    query2q = mxq(f64(query2), 0, "e4m3")
    notesidx2q = mxq(f64(notes)[:, idx2], 0, "e4m3")
    b = query2q.T @ notesidx2q
    g1 = sigmoid(b)
    s = a * g1 + (1.0 - g1) * f64(lam)
    p = np.exp(s - np.max(s, axis=1, keepdims=True))
    r = p / np.sum(p, axis=1, keepdims=True)
    rt = r.T
    rg = rt.reshape(I, K, Q // K).sum(axis=2)
    rq = 1.0 / np.sqrt(rg)
    rr = np.repeat(rq, Q // K, axis=1)
    w0 = rt * rr
    w = w0.T
    wo1 = w * f64(os)
    wt1 = wo1.T
    vt1 = f64(vals)[:, idx].T
    wt1q = mxq(wt1, 0, "e4m3")
    vt1q = mxq(vt1, 0, "e4m3")
    o = wt1q.T @ vt1q
    rs = f64(target) - o
    k2 = np.sqrt(np.mean(np.square(rs), axis=1, keepdims=True) + 0.5)
    y = rs / k2
    return y

@@ -1,0 +1,178 @@
+from contextlib import ExitStack
+
+import concourse.mybir as mybir
+from concourse.masks import make_identity
+
+D, T, I, Q, E, U, K = 512, 2048, 512, 128, 512, 1024, 16
+FLOPS = 2 * Q * I * D * 2 + 2 * Q * E * I
+
+F32 = mybir.dt.float32
+BF16 = mybir.dt.bfloat16
+I32 = mybir.dt.int32
+U32 = mybir.dt.uint32
+U16 = mybir.dt.uint16
+U8 = mybir.dt.uint8
+FP8X4 = mybir.dt.float8_e4m3fn_x4
+FP4X4 = mybir.dt.float4_e2m1fn_x4
+ACT = mybir.ActivationFunctionType
+ALU = mybir.AluOpType
+AX = mybir.AxisListType
+
+P = 128
+PACK = 4
+GROUP = Q // K
+TINY = 1e-30
+WEAVE_SPLIT = 320
+
+
+def tile_attend_tilted_balanced_remainder_kernel(tc, query, query2, keys_words, keys_scales, notes, lam, factor, vals, target, offs, offs2, out):
+    nc = tc.nc
+    with ExitStack() as ctx:
+        lists = ctx.enter_context(tc.tile_pool(name="lists", bufs=1))
+        sb = ctx.enter_context(tc.tile_pool(name="sb", bufs=1))
+        psum = ctx.enter_context(tc.psum_pool(name="psum", bufs=1))
+
+        offs_t = lists.tile([P, I // 16], U16, name="offs_t")
+        offs2_t = lists.tile([P, I // 16], U16, name="offs2_t")
+        kw = sb.tile([P, T], U16, name="kw", align_bytes=64)
+        ks = sb.tile([P, T], U8, name="ks", align_bytes=64)
+        q2_raw = sb.tile([P, PACK, Q], F32, name="q2_raw")
+        q_raw = sb.tile([P, PACK, Q], F32, name="q_raw")
+        planes = [sb.tile([P, U], F32, name="note%d" % t) for t in range(PACK)]
+        vblocks = [sb.tile([P, T], F32, name="val%d" % b, tag="val%d" % b) for b in range(E // P)]
+        lam_t = sb.tile([P, 1], F32, name="lam_t")
+        os_t = sb.tile([P, PACK], F32, name="os_t")
+        tgt = sb.tile([P, E], F32, name="tgt")
+        ident = sb.tile([P, P], F32, name="ident")
+
+        nc.gpsimd.memset(ks[:].bitcast(I32), 0)
+        notes_v = notes.rearrange("(p j) u -> p j u", j=PACK)
+        nc.sync.dma_start(offs_t[:], offs)
+        nc.sync.dma_start(out=kw[:].bitcast(I32), in_=keys_words[0].bitcast(I32))
+        nc.sync.dma_start(offs2_t[:], offs2)
+        nc.sync.dma_start(out=q2_raw[:], in_=query2.rearrange("(p j) w -> p j w", j=PACK))
+        for t in range(2):
+            nc.sync.dma_start(out=planes[t][:], in_=notes_v[:, t, :])
+        for g in range(4):
+            nc.sync.dma_start(out=ks[32 * g : 32 * g + 4, :].bitcast(I32), in_=keys_scales[0, 4 * g : 4 * g + 4, :].bitcast(I32))
+        for t in range(2, PACK):
+            nc.sync.dma_start(out=planes[t][:], in_=notes_v[:, t, :])
+        nc.sync.dma_start(out=q_raw[:], in_=query.rearrange("(p j) w -> p j w", j=PACK))
+        nc.sync.dma_start(out=lam_t[:], in_=lam)
+        nc.sync.dma_start(out=os_t[:], in_=factor.rearrange("o (p t) -> (o p) t", t=PACK))
+        for b in range(E // P):
+            nc.sync.dma_start(out=vblocks[b][:], in_=vals[b * P : (b + 1) * P, :])
+        nc.sync.dma_start(out=tgt[:], in_=target)
+        make_identity(nc, ident[:])
+
+        kwg = sb.tile([P, I], U16, name="kwg", align_bytes=64)
+        ksg = sb.tile([P, I], U8, name="ksg", align_bytes=64)
+        nc.vector.tensor_copy(kwg[:], kw[:].indirect(offs_t[:]))
+        nc.vector.tensor_copy(ksg[:], ks[:].indirect(offs_t[:]))
+
+        def quantise_queries(raw, name, copy):
+            woven = sb.tile([P, Q, PACK], BF16, name=name + "_woven", align_bytes=64)
+            codes = sb.tile([P, Q], U32, name=name + "_codes", align_bytes=64)
+            scales = sb.tile([P, Q], U8, name=name + "_scales", align_bytes=64)
+            copy(out=woven[:].rearrange("p (c i) t -> p c t i", i=4), in_=raw[:].rearrange("p t (c i) -> p c t i", i=4))
+            nc.vector.quantize_mx(out=codes[:].bitcast(FP8X4), scales=scales[:], in_=woven[:].rearrange("p w j -> p (w j)"))
+            return codes, scales
+
+        q2c, q2s = quantise_queries(q2_raw, "q2", nc.scalar.copy)
+
+        ng = sb.tile([P, PACK, I], BF16, name="ng", align_bytes=64)
+        for t in range(PACK):
+            nc.vector.tensor_copy(ng[:, t, :], planes[t][:].indirect(offs2_t[:]))
+        nw = sb.tile([P, I, PACK], BF16, name="nw", align_bytes=64)
+        nw_v = nw[:].rearrange("p (c i) t -> p c t i", i=4)
+        ng_v = ng[:].rearrange("p t (c i) -> p c t i", i=4)
+        cs = WEAVE_SPLIT // 4
+        nc.vector.tensor_copy(out=nw_v[:, :cs], in_=ng_v[:, :cs])
+        nc.scalar.copy(out=nw_v[:, cs:], in_=ng_v[:, cs:])
+        ncodes = sb.tile([P, I], U32, name="ncodes", align_bytes=64)
+        nscales = sb.tile([P, I], U8, name="nscales", align_bytes=64)
+        nc.vector.quantize_mx(out=ncodes[:].bitcast(FP8X4), scales=nscales[:], in_=nw[:].rearrange("p w j -> p (w j)"))
+
+        qc, qs = quantise_queries(q_raw, "q", nc.scalar.copy)
+
+        a_ps = psum.tile([P, I], F32, name="a_ps")
+        b_ps = psum.tile([P, I], F32, name="b_ps")
+        nc.tensor.matmul_mx(out=a_ps[:], lhsT=qc[:].bitcast(FP8X4), lhsT_scale=qs[:], rhs=kwg[:].bitcast(FP4X4), rhs_scale=ksg[:], start=True, stop=True)
+        nc.tensor.matmul_mx(out=b_ps[:], lhsT=q2c[:].bitcast(FP8X4), lhsT_scale=q2s[:], rhs=ncodes[:].bitcast(FP8X4), rhs_scale=nscales[:], start=True, stop=True)
+
+        vcodes = sb.tile([P, E], U32, name="vcodes", align_bytes=64)
+        vscales = sb.tile([P, E], U8, name="vscales", align_bytes=64)
+
+        def value_block(b):
+            vg = sb.tile([P, I], BF16, name="vg%d" % b, align_bytes=64)
+            nc.vector.tensor_copy(vg[:], vblocks[b][:].indirect(offs_t[:]))
+            words = vg[:].bitcast(F32)
+            vt_ps = psum.tile([P, 2, P], F32, name="vt_ps", bufs=2)
+            for u in range(2):
+                nc.tensor.transpose(vt_ps[:, u, :], words[:, u : I // 2 : 2], ident[:])
+            vw = sb.tile([P, P, PACK], BF16, name="vw%d" % b, align_bytes=64)
+            nc.scalar.copy(out=vw[:].bitcast(F32), in_=vt_ps[:].rearrange("p u e -> p e u"))
+            return vw
+
+        def quantise_values(b, vw):
+            nc.vector.quantize_mx(out=vcodes[:, b * P : (b + 1) * P].bitcast(FP8X4), scales=vscales[:, b * P : (b + 1) * P], in_=vw[:].rearrange("p e j -> p (e j)"))
+
+        am = sb.tile([P, PACK, P], F32, name="am")
+        th = sb.tile([P, PACK, P], F32, name="th")
+        nc.scalar.activation(out=am[:], in_=a_ps[:].rearrange("q (p t) -> q t p", t=PACK), func=ACT.Identity, bias=lam_t[:], scale=-1.0)
+        nc.scalar.activation(out=th[:], in_=b_ps[:].rearrange("q (p t) -> q t p", t=PACK), func=ACT.Tanh, scale=0.5)
+        vw0 = value_block(0)
+        z = sb.tile([P, I], F32, name="z", tag="val0")
+        nc.vector.scalar_tensor_tensor(out=z[:], in0=th[:].rearrange("q t p -> q (t p)"), scalar=1.0, in1=am[:].rearrange("q t p -> q (t p)"), op0=ALU.add, op1=ALU.mult)
+        zh = sb.tile([P, I], F32, name="zh")
+        zmin = sb.tile([P, 1], F32, name="zmin")
+        nc.vector.tensor_scalar(out=zh[:], in0=z[:], scalar1=0.5, scalar2=None, op0=ALU.mult, op1=ALU.min, accum_out=zmin[:])
+        pexp = sb.tile([P, I], F32, name="pexp")
+        psumr = sb.tile([P, 1], F32, name="psumr")
+        nc.scalar.activation(out=pexp[:], in_=zh[:], func=ACT.Exp, bias=zmin[:], scale=-1.0, accum_out=psumr[:])
+        warm = sb.tile([P, 1], F32, name="warm")
+        nc.scalar.activation(out=warm[:], in_=psumr[:], func=ACT.Abs_reciprocal_sqrt)
+        vw1 = value_block(1)
+        rinv = sb.tile([P, 1], F32, name="rinv", tag="val1")
+        nc.vector.reciprocal(rinv[:], psumr[:])
+        r = sb.tile([P, I], F32, name="r")
+        nc.vector.tensor_scalar(out=r[:], in0=pexp[:], scalar1=rinv[:], scalar2=TINY, op0=ALU.mult, op1=ALU.max)
+        rt_ps = psum.tile([P, PACK, Q], F32, name="rt_ps")
+        for t in range(PACK):
+            nc.tensor.transpose(rt_ps[:, t, :], r[:, t * P : (t + 1) * P], ident[:])
+        vw2 = value_block(2)
+        rg = sb.tile([P, K, PACK], F32, name="rg", tag="val2")
+        nc.vector.tensor_reduce(out=rg[:], in_=rt_ps[:].rearrange("p t (k j) -> p k t j", j=GROUP), axis=AX.X, op=ALU.add)
+        rq = sb.tile([P, K, PACK], F32, name="rq")
+        nc.scalar.activation(out=rq[:], in_=rg[:], func=ACT.Abs_reciprocal_sqrt)
+
+        quantise_values(0, vw0)
+        quantise_values(1, vw1)
+        c = sb.tile([P, K, PACK], F32, name="c")
+        nc.vector.tensor_tensor(out=c[:], in0=rq[:], in1=os_t[:].unsqueeze(1).broadcast_to([P, K, PACK]), op=ALU.mult)
+        ww = sb.tile([P, Q, PACK], BF16, name="ww", align_bytes=64)
+        nc.vector.tensor_tensor(
+            out=ww[:].rearrange("p (k j) t -> p k j t", j=GROUP),
+            in0=rt_ps[:].rearrange("p t (k j) -> p k j t", j=GROUP),
+            in1=c[:].unsqueeze(2).broadcast_to([P, K, GROUP, PACK]),
+            op=ALU.mult,
+        )
+        quantise_values(2, vw2)
+        vw3 = value_block(3)
+        wcodes = sb.tile([P, Q], U32, name="wcodes", align_bytes=64)
+        wscales = sb.tile([P, Q], U8, name="wscales", align_bytes=64)
+        nc.vector.quantize_mx(out=wcodes[:].bitcast(FP8X4), scales=wscales[:], in_=ww[:].rearrange("p w j -> p (w j)"))
+
+        quantise_values(3, vw3)
+        o_ps = psum.tile([P, E], F32, name="o_ps")
+        nc.tensor.matmul_mx(out=o_ps[:], lhsT=wcodes[:].bitcast(FP8X4), lhsT_scale=wscales[:], rhs=vcodes[:].bitcast(FP8X4), rhs_scale=vscales[:], start=True, stop=True)
+        rs = sb.tile([P, E], F32, name="rs")
+        nc.vector.tensor_tensor(out=rs[:], in0=tgt[:], in1=o_ps[:], op=ALU.subtract)
+        sq = sb.tile([P, E], F32, name="sq")
+        ssq = sb.tile([P, 1], F32, name="ssq")
+        nc.scalar.activation(out=sq[:], in_=rs[:], func=ACT.Square, accum_out=ssq[:])
+        kinv = sb.tile([P, 1], F32, name="kinv")
+        nc.scalar.activation(out=kinv[:], in_=ssq[:], func=ACT.Abs_reciprocal_sqrt, scale=1.0 / E, bias=0.5)
+        y = sb.tile([P, E], F32, name="y")
+        nc.vector.tensor_scalar(out=y[:], in0=rs[:], scalar1=kinv[:], scalar2=None, op0=ALU.mult)
+        nc.sync.dma_start(out=out, in_=y[:])

@@ -21,8 +21,7 @@ AX = mybir.AxisListType
 P = 128
 PACK = 4
 GROUP = Q // K
-TINY = 1e-30
-WEAVE_SPLIT = 320
+TINY = 2.0**-100
 
 
 def tile_attend_tilted_balanced_remainder_kernel(tc, query, query2, keys_words, keys_scales, notes, lam, factor, vals, target, offs, offs2, out):
@@ -36,10 +35,10 @@ def tile_attend_tilted_balanced_remainder_kernel(tc, query, query2, keys_words, 
         offs2_t = lists.tile([P, I // 16], U16, name="offs2_t")
         kw = sb.tile([P, T], U16, name="kw", align_bytes=64)
         ks = sb.tile([P, T], U8, name="ks", align_bytes=64)
-        q2_raw = sb.tile([P, PACK, Q], F32, name="q2_raw")
+        q2_raw = sb.tile([P, PACK, Q], F32, name="q2_raw", tag="nw1", align_bytes=64)
         q_raw = sb.tile([P, PACK, Q], F32, name="q_raw")
         planes = [sb.tile([P, U], F32, name="note%d" % t) for t in range(PACK)]
-        vblocks = [sb.tile([P, T], F32, name="val%d" % b, tag="val%d" % b) for b in range(E // P)]
+        vblocks = [sb.tile([P, T], F32, name="val%d" % b, tag="val%d" % b, align_bytes=64) for b in range(E // P)]
         lam_t = sb.tile([P, 1], F32, name="lam_t")
         os_t = sb.tile([P, PACK], F32, name="os_t")
         tgt = sb.tile([P, E], F32, name="tgt")
@@ -48,26 +47,31 @@ def tile_attend_tilted_balanced_remainder_kernel(tc, query, query2, keys_words, 
         nc.gpsimd.memset(ks[:].bitcast(I32), 0)
         notes_v = notes.rearrange("(p j) u -> p j u", j=PACK)
         nc.sync.dma_start(offs_t[:], offs)
-        nc.sync.dma_start(out=kw[:].bitcast(I32), in_=keys_words[0].bitcast(I32))
+        for h in range(2):
+            cols = slice(h * T // 4, (h + 1) * T // 4)
+            nc.sync.dma_start(out=kw[:].bitcast(I32)[:, cols], in_=keys_words[0].bitcast(I32)[:, cols])
         nc.sync.dma_start(offs2_t[:], offs2)
-        nc.sync.dma_start(out=q2_raw[:], in_=query2.rearrange("(p j) w -> p j w", j=PACK))
-        for t in range(2):
-            nc.sync.dma_start(out=planes[t][:], in_=notes_v[:, t, :])
+        nc.scalar.dma_start(out=lam_t[:], in_=lam)
+        nc.scalar.dma_start(out=os_t[:], in_=factor.rearrange("o (p t) -> (o p) t", t=PACK))
+        nc.sync.dma_start(out=planes[0][:], in_=notes_v[:, 0, :])
+        nc.sync.dma_start(out=q_raw[:], in_=query.rearrange("(p j) w -> p j w", j=PACK))
         for g in range(4):
             nc.sync.dma_start(out=ks[32 * g : 32 * g + 4, :].bitcast(I32), in_=keys_scales[0, 4 * g : 4 * g + 4, :].bitcast(I32))
-        for t in range(2, PACK):
+        for t in range(1, PACK):
             nc.sync.dma_start(out=planes[t][:], in_=notes_v[:, t, :])
-        nc.sync.dma_start(out=q_raw[:], in_=query.rearrange("(p j) w -> p j w", j=PACK))
-        nc.sync.dma_start(out=lam_t[:], in_=lam)
-        nc.sync.dma_start(out=os_t[:], in_=factor.rearrange("o (p t) -> (o p) t", t=PACK))
+        nc.sync.dma_start(out=q2_raw[:], in_=query2.rearrange("(p j) w -> p j w", j=PACK))
         for b in range(E // P):
             nc.sync.dma_start(out=vblocks[b][:], in_=vals[b * P : (b + 1) * P, :])
         nc.sync.dma_start(out=tgt[:], in_=target)
         make_identity(nc, ident[:])
+        floor = sb.tile([P, 1], F32, name="floor", tag="floor", align_bytes=64)
+        nc.gpsimd.memset(floor[:], TINY)
 
         kwg = sb.tile([P, I], U16, name="kwg", align_bytes=64)
         ksg = sb.tile([P, I], U8, name="ksg", align_bytes=64)
         nc.vector.tensor_copy(kwg[:], kw[:].indirect(offs_t[:]))
+        ng = sb.tile([P, PACK, I], BF16, name="ng", tag="ng", align_bytes=64)
+        nc.vector.tensor_copy(ng[:, 0, :], planes[0][:].indirect(offs2_t[:]))
         nc.vector.tensor_copy(ksg[:], ks[:].indirect(offs_t[:]))
 
         def quantise_queries(raw, name, copy):
@@ -78,101 +82,124 @@ def tile_attend_tilted_balanced_remainder_kernel(tc, query, query2, keys_words, 
             nc.vector.quantize_mx(out=codes[:].bitcast(FP8X4), scales=scales[:], in_=woven[:].rearrange("p w j -> p (w j)"))
             return codes, scales
 
-        q2c, q2s = quantise_queries(q2_raw, "q2", nc.scalar.copy)
-
-        ng = sb.tile([P, PACK, I], BF16, name="ng", align_bytes=64)
-        for t in range(PACK):
-            nc.vector.tensor_copy(ng[:, t, :], planes[t][:].indirect(offs2_t[:]))
-        nw = sb.tile([P, I, PACK], BF16, name="nw", align_bytes=64)
-        nw_v = nw[:].rearrange("p (c i) t -> p c t i", i=4)
-        ng_v = ng[:].rearrange("p t (c i) -> p c t i", i=4)
-        cs = WEAVE_SPLIT // 4
-        nc.vector.tensor_copy(out=nw_v[:, :cs], in_=ng_v[:, :cs])
-        nc.scalar.copy(out=nw_v[:, cs:], in_=ng_v[:, cs:])
-        ncodes = sb.tile([P, I], U32, name="ncodes", align_bytes=64)
-        nscales = sb.tile([P, I], U8, name="nscales", align_bytes=64)
-        nc.vector.quantize_mx(out=ncodes[:].bitcast(FP8X4), scales=nscales[:], in_=nw[:].rearrange("p w j -> p (w j)"))
-
         qc, qs = quantise_queries(q_raw, "q", nc.scalar.copy)
-
-        a_ps = psum.tile([P, I], F32, name="a_ps")
-        b_ps = psum.tile([P, I], F32, name="b_ps")
+        a_ps = psum.tile([P, I], F32, name="a_ps", tag="a")
         nc.tensor.matmul_mx(out=a_ps[:], lhsT=qc[:].bitcast(FP8X4), lhsT_scale=qs[:], rhs=kwg[:].bitcast(FP4X4), rhs_scale=ksg[:], start=True, stop=True)
-        nc.tensor.matmul_mx(out=b_ps[:], lhsT=q2c[:].bitcast(FP8X4), lhsT_scale=q2s[:], rhs=ncodes[:].bitcast(FP8X4), rhs_scale=nscales[:], start=True, stop=True)
 
-        vcodes = sb.tile([P, E], U32, name="vcodes", align_bytes=64)
-        vscales = sb.tile([P, E], U8, name="vscales", align_bytes=64)
+        nb = sb.tile([P, U], BF16, name="nb", tag="nb")
+        nc.scalar.activation(out=nb[:], in_=planes[1][:], func=ACT.Copy)
+        nc.scalar.activation(out=ng[:, 1, :], in_=nb[:].indirect(offs2_t[:]), func=ACT.Copy)
+        for t in range(2, PACK):
+            nc.vector.tensor_copy(ng[:, t, :], planes[t][:].indirect(offs2_t[:]))
+        HI = I // 2
+        nw = [sb.tile([P, HI, PACK], BF16, name="nw%d" % h, tag="nw%d" % h, align_bytes=64) for h in range(2)]
+        for h, copy in enumerate((nc.vector.tensor_copy, nc.scalar.copy)):
+            copy(out=nw[h][:].rearrange("p (c i) t -> p c t i", i=4), in_=ng[:, :, h * HI : (h + 1) * HI].rearrange("p t (c i) -> p c t i", i=4))
+            if h == 0:
+                q2c, q2s = quantise_queries(q2_raw, "q2", nc.scalar.copy)
+        b_ps = []
+        for h in range(2):
+            ncodes = sb.tile([P, HI], U32, name="ncodes%d" % h, align_bytes=64)
+            nscales = sb.tile([P, HI], U8, name="nscales%d" % h, align_bytes=64)
+            nc.vector.quantize_mx(out=ncodes[:].bitcast(FP8X4), scales=nscales[:], in_=nw[h][:].rearrange("p w j -> p (w j)"))
+            b_ps.append(psum.tile([P, HI], F32, name="b_ps%d" % h, tag="b%d" % h))
+            nc.tensor.matmul_mx(out=b_ps[h][:], lhsT=q2c[:].bitcast(FP8X4), lhsT_scale=q2s[:], rhs=ncodes[:].bitcast(FP8X4), rhs_scale=nscales[:], start=True, stop=True)
 
-        def value_block(b):
-            vg = sb.tile([P, I], BF16, name="vg%d" % b, align_bytes=64)
+        def value_block(b, gathered_tag, vt_ps):
+            vg = sb.tile([P, I], BF16, name="vg%d" % b, tag=gathered_tag, align_bytes=64)
             nc.vector.tensor_copy(vg[:], vblocks[b][:].indirect(offs_t[:]))
             words = vg[:].bitcast(F32)
-            vt_ps = psum.tile([P, 2, P], F32, name="vt_ps", bufs=2)
             for u in range(2):
                 nc.tensor.transpose(vt_ps[:, u, :], words[:, u : I // 2 : 2], ident[:])
-            vw = sb.tile([P, P, PACK], BF16, name="vw%d" % b, align_bytes=64)
-            nc.scalar.copy(out=vw[:].bitcast(F32), in_=vt_ps[:].rearrange("p u e -> p e u"))
-            return vw
 
-        def quantise_values(b, vw):
-            nc.vector.quantize_mx(out=vcodes[:, b * P : (b + 1) * P].bitcast(FP8X4), scales=vscales[:, b * P : (b + 1) * P], in_=vw[:].rearrange("p e j -> p (e j)"))
+        def weave_values(vw, vt_ps):
+            nc.scalar.copy(out=vw.bitcast(F32), in_=vt_ps.rearrange("p u e -> p e u"))
 
-        am = sb.tile([P, PACK, P], F32, name="am")
+        def quantise(codes, scales, woven):
+            nc.vector.quantize_mx(out=codes.bitcast(FP8X4), scales=scales, in_=woven.rearrange("p e j -> p (e j)"))
+
+        am = sb.tile([P, PACK, P], F32, name="am", tag="ng", align_bytes=64)
         th = sb.tile([P, PACK, P], F32, name="th")
         nc.scalar.activation(out=am[:], in_=a_ps[:].rearrange("q (p t) -> q t p", t=PACK), func=ACT.Identity, bias=lam_t[:], scale=-1.0)
-        nc.scalar.activation(out=th[:], in_=b_ps[:].rearrange("q (p t) -> q t p", t=PACK), func=ACT.Tanh, scale=0.5)
-        vw0 = value_block(0)
-        z = sb.tile([P, I], F32, name="z", tag="val0")
-        nc.vector.scalar_tensor_tensor(out=z[:], in0=th[:].rearrange("q t p -> q (t p)"), scalar=1.0, in1=am[:].rearrange("q t p -> q (t p)"), op0=ALU.add, op1=ALU.mult)
-        zh = sb.tile([P, I], F32, name="zh")
+        for h in range(2):
+            nc.scalar.activation(out=th[:, :, h * P // 2 : (h + 1) * P // 2], in_=b_ps[h][:].rearrange("q (p t) -> q t p", t=PACK), func=ACT.Tanh, scale=0.5)
+        vt0 = psum.tile([P, 2, P], F32, name="vt0", tag="vt")
+        value_block(0, "nw1", vt0[:])
+        z = sb.tile([P, I], F32, name="z", tag="val0", align_bytes=64)
+        z_v = z[:].rearrange("q (t p) -> q t p", t=PACK)
+        for h in range(2):
+            cols = slice(h * P // 2, (h + 1) * P // 2)
+            nc.vector.scalar_tensor_tensor(out=z_v[:, :, cols], in0=th[:, :, cols], scalar=1.0, in1=am[:, :, cols], op0=ALU.add, op1=ALU.mult)
+        zh = sb.tile([P, I], F32, name="zh", tag="zh", align_bytes=64)
         zmin = sb.tile([P, 1], F32, name="zmin")
         nc.vector.tensor_scalar(out=zh[:], in0=z[:], scalar1=0.5, scalar2=None, op0=ALU.mult, op1=ALU.min, accum_out=zmin[:])
-        pexp = sb.tile([P, I], F32, name="pexp")
-        psumr = sb.tile([P, 1], F32, name="psumr")
+        pexp = sb.tile([P, I], F32, name="pexp", tag="pexp", align_bytes=64)
+        psumr = sb.tile([P, 1], F32, name="psumr", tag="psumr", align_bytes=64)
         nc.scalar.activation(out=pexp[:], in_=zh[:], func=ACT.Exp, bias=zmin[:], scale=-1.0, accum_out=psumr[:])
-        warm = sb.tile([P, 1], F32, name="warm")
-        nc.scalar.activation(out=warm[:], in_=psumr[:], func=ACT.Abs_reciprocal_sqrt)
-        vw1 = value_block(1)
-        rinv = sb.tile([P, 1], F32, name="rinv", tag="val1")
+        vt1 = psum.tile([P, 2, P], F32, name="vt1", tag="a")
+        value_block(1, "val0", vt1[:])
+        vw0 = sb.tile([P, P, PACK], BF16, name="vw0", tag="zh", align_bytes=64)
+        weave_values(vw0[:], vt0[:])
+        rinv = sb.tile([P, 1], F32, name="rinv", tag="val1", align_bytes=64)
         nc.vector.reciprocal(rinv[:], psumr[:])
         r = sb.tile([P, I], F32, name="r")
-        nc.vector.tensor_scalar(out=r[:], in0=pexp[:], scalar1=rinv[:], scalar2=TINY, op0=ALU.mult, op1=ALU.max)
+        for h in range(2):
+            cols = slice(h * HI, (h + 1) * HI)
+            nc.scalar.activation(out=r[:, cols], in_=pexp[:, cols], func=ACT.Copy, scale=rinv[:])
+        vw1 = sb.tile([P, P, PACK], BF16, name="vw1", tag="pexp", align_bytes=64)
+        weave_values(vw1[:], vt1[:])
+        warm = sb.tile([P, 1], F32, name="warm")
+        nc.scalar.activation(out=warm[:], in_=r[:, I - 1 :], func=ACT.Abs_reciprocal_sqrt, bias=floor[:])
         rt_ps = psum.tile([P, PACK, Q], F32, name="rt_ps")
         for t in range(PACK):
             nc.tensor.transpose(rt_ps[:, t, :], r[:, t * P : (t + 1) * P], ident[:])
-        vw2 = value_block(2)
-        rg = sb.tile([P, K, PACK], F32, name="rg", tag="val2")
-        nc.vector.tensor_reduce(out=rg[:], in_=rt_ps[:].rearrange("p t (k j) -> p k t j", j=GROUP), axis=AX.X, op=ALU.add)
+        vt23 = psum.tile([P, 2, 2, P], F32, name="vt23", tag="a")
+        value_block(2, "psumr", vt23[:, 0])
+        value_block(3, "vg3", vt23[:, 1])
+        rg = sb.tile([P, K, PACK], F32, name="rg", tag="val3", align_bytes=64)
+        vscales = [sb.tile([P, 2 * P], U8, name="vscales%d" % h, align_bytes=64) for h in range(2)]
+        rto = sb.tile([P, K, GROUP, PACK], F32, name="rto")
         rq = sb.tile([P, K, PACK], F32, name="rq")
-        nc.scalar.activation(out=rq[:], in_=rg[:], func=ACT.Abs_reciprocal_sqrt)
-
-        quantise_values(0, vw0)
-        quantise_values(1, vw1)
-        c = sb.tile([P, K, PACK], F32, name="c")
-        nc.vector.tensor_tensor(out=c[:], in0=rq[:], in1=os_t[:].unsqueeze(1).broadcast_to([P, K, PACK]), op=ALU.mult)
         ww = sb.tile([P, Q, PACK], BF16, name="ww", align_bytes=64)
-        nc.vector.tensor_tensor(
-            out=ww[:].rearrange("p (k j) t -> p k j t", j=GROUP),
-            in0=rt_ps[:].rearrange("p t (k j) -> p k j t", j=GROUP),
-            in1=c[:].unsqueeze(2).broadcast_to([P, K, GROUP, PACK]),
-            op=ALU.mult,
-        )
-        quantise_values(2, vw2)
-        vw3 = value_block(3)
+        ww_v = ww[:].rearrange("p (k j) t -> p k j t", j=GROUP)
+        halves = [slice(h * K // 2, (h + 1) * K // 2) for h in range(2)]
+        for ks_ in halves:
+            nc.vector.tensor_reduce(out=rg[:, ks_], in_=rt_ps[:].rearrange("p t (k j) -> p k t j", j=GROUP)[:, ks_], axis=AX.X, op=ALU.add)
+            nc.scalar.activation(out=rq[:, ks_], in_=rg[:, ks_], func=ACT.Abs_reciprocal_sqrt, bias=floor[:])
+        for ks_ in halves:
+            nc.vector.tensor_tensor(out=rto[:, ks_], in0=rt_ps[:].rearrange("p t (k j) -> p k j t", j=GROUP)[:, ks_], in1=os_t[:].unsqueeze(1).unsqueeze(1).broadcast_to([P, K // 2, GROUP, PACK]), op=ALU.mult)
+        vw23 = sb.tile([P, 2, P, PACK], BF16, name="vw23", tag="floor", align_bytes=64)
+        nc.scalar.copy(out=vw23[:].bitcast(F32), in_=vt23[:].rearrange("p b u e -> p b e u"))
+        for ks_ in halves:
+            nc.vector.tensor_tensor(out=ww_v[:, ks_], in0=rto[:, ks_], in1=rq[:, ks_].unsqueeze(2).broadcast_to([P, K // 2, GROUP, PACK]), op=ALU.mult)
+        vcodes = [sb.tile([P, 2 * P], U32, name="vcodes0", tag="val3", align_bytes=64), sb.tile([P, 2 * P], U32, name="vcodes1", align_bytes=64)]
+        quantise(vcodes[0][:, :P], vscales[0][:, :P], vw0[:])
+        quantise(vcodes[0][:, P:], vscales[0][:, P:], vw1[:])
         wcodes = sb.tile([P, Q], U32, name="wcodes", align_bytes=64)
         wscales = sb.tile([P, Q], U8, name="wscales", align_bytes=64)
-        nc.vector.quantize_mx(out=wcodes[:].bitcast(FP8X4), scales=wscales[:], in_=ww[:].rearrange("p w j -> p (w j)"))
+        quantise(wcodes[:], wscales[:], ww[:])
+        quantise(vcodes[1][:], vscales[1][:], vw23[:].rearrange("p b e j -> p (b e) j"))
 
-        quantise_values(3, vw3)
-        o_ps = psum.tile([P, E], F32, name="o_ps")
-        nc.tensor.matmul_mx(out=o_ps[:], lhsT=wcodes[:].bitcast(FP8X4), lhsT_scale=wscales[:], rhs=vcodes[:].bitcast(FP8X4), rhs_scale=vscales[:], start=True, stop=True)
-        rs = sb.tile([P, E], F32, name="rs")
-        nc.vector.tensor_tensor(out=rs[:], in0=tgt[:], in1=o_ps[:], op=ALU.subtract)
-        sq = sb.tile([P, E], F32, name="sq")
-        ssq = sb.tile([P, 1], F32, name="ssq")
-        nc.scalar.activation(out=sq[:], in_=rs[:], func=ACT.Square, accum_out=ssq[:])
+        H = E // 2
+        rs_a = sb.tile([P, H + 1], F32, name="rs_a")
+        rs_b = sb.tile([P, H], F32, name="rs_b")
+        nc.gpsimd.memset(rs_a[:, H : H + 1], 16.0)
+        for h, rs in enumerate((rs_a, rs_b)):
+            o_ps = psum.tile([P, H], F32, name="o_ps%d" % h)
+            cols = slice(h * H, (h + 1) * H)
+            nc.tensor.matmul_mx(out=o_ps[:], lhsT=wcodes[:].bitcast(FP8X4), lhsT_scale=wscales[:], rhs=vcodes[h][:, :].bitcast(FP8X4), rhs_scale=vscales[h][:], start=True, stop=True)
+            nc.vector.tensor_tensor(out=rs[:, :H], in0=tgt[:, cols], in1=o_ps[:], op=ALU.subtract)
+        sq_a = sb.tile([P, H + 1], F32, name="sq_a")
+        sq_b = sb.tile([P, H], F32, name="sq_b")
+        ssq_a = sb.tile([P, 1], F32, name="ssq_a")
+        ssq_b = sb.tile([P, 1], F32, name="ssq_b")
+        nc.scalar.activation(out=sq_a[:], in_=rs_a[:], func=ACT.Square, accum_out=ssq_a[:])
+        nc.vector.scalar_tensor_tensor(out=sq_b[:], in0=rs_b[:], scalar=1.0 / E, in1=rs_b[:], op0=ALU.mult, op1=ALU.mult, accum_out=ssq_b[:])
         kinv = sb.tile([P, 1], F32, name="kinv")
-        nc.scalar.activation(out=kinv[:], in_=ssq[:], func=ACT.Abs_reciprocal_sqrt, scale=1.0 / E, bias=0.5)
-        y = sb.tile([P, E], F32, name="y")
-        nc.vector.tensor_scalar(out=y[:], in0=rs[:], scalar1=kinv[:], scalar2=None, op0=ALU.mult)
-        nc.sync.dma_start(out=out, in_=y[:])
+        nc.scalar.activation(out=kinv[:], in_=ssq_a[:], func=ACT.Abs_reciprocal_sqrt, scale=1.0 / E, bias=ssq_b[:])
+        y_a = sb.tile([P, H], F32, name="y_a")
+        y_b = sb.tile([P, H], F32, name="y_b")
+        nc.vector.tensor_scalar(out=y_a[:], in0=rs_a[:, :H], scalar1=kinv[:], scalar2=None, op0=ALU.mult)
+        nc.sync.dma_start(out=out[:, :H], in_=y_a[:])
+        nc.scalar.activation(out=y_b[:], in_=rs_b[:], func=ACT.Copy, scale=kinv[:])
+        nc.scalar.dma_start(out=out[:, H:], in_=y_b[:])

@@ -20,8 +20,15 @@ AX = mybir.AxisListType
 
 P = 128
 PACK = 4
+QUADRANTS = 4
+LIST_COLUMNS = I // 16
 GROUP = Q // K
-TINY = 2.0**-100
+HALF_SLOTS = I // 2
+HALF_FEATURES = E // 2
+RUN = 4
+ALIGN = 64
+SUM_FLOOR = 2.0**-100
+PAD_VALUE = 16.0
 
 
 def tile_attend_tilted_balanced_remainder_kernel(tc, query, query2, keys_words, keys_scales, notes, lam, factor, vals, target, offs, offs2, out):
@@ -31,175 +38,187 @@ def tile_attend_tilted_balanced_remainder_kernel(tc, query, query2, keys_words, 
         sb = ctx.enter_context(tc.tile_pool(name="sb", bufs=1))
         psum = ctx.enter_context(tc.psum_pool(name="psum", bufs=1))
 
-        offs_t = lists.tile([P, I // 16], U16, name="offs_t")
-        offs2_t = lists.tile([P, I // 16], U16, name="offs2_t")
-        kw = sb.tile([P, T], U16, name="kw", align_bytes=64)
-        ks = sb.tile([P, T], U8, name="ks", align_bytes=64)
-        q2_raw = sb.tile([P, PACK, Q], F32, name="q2_raw", tag="nw1", align_bytes=64)
+        def quantise(codes, scales, woven):
+            nc.vector.quantize_mx(out=codes.bitcast(FP8X4), scales=scales, in_=woven.rearrange("p c t -> p (c t)"))
+
+        def weave(copy, woven, by_place):
+            copy(out=woven.rearrange("p (c i) t -> p c t i", i=RUN), in_=by_place.rearrange("p t (c i) -> p c t i", i=RUN))
+
+        offs_t = lists.tile([P, LIST_COLUMNS], U16, name="offs_t")
+        offs2_t = lists.tile([P, LIST_COLUMNS], U16, name="offs2_t")
+        key_words = sb.tile([P, T], U16, name="key_words", align_bytes=ALIGN)
+        key_scales = sb.tile([P, T], U8, name="key_scales", align_bytes=ALIGN)
+        q2_raw = sb.tile([P, PACK, Q], F32, name="q2_raw", tag="q2_raw", align_bytes=ALIGN)
         q_raw = sb.tile([P, PACK, Q], F32, name="q_raw")
-        planes = [sb.tile([P, U], F32, name="note%d" % t) for t in range(PACK)]
-        vblocks = [sb.tile([P, T], F32, name="val%d" % b, tag="val%d" % b, align_bytes=64) for b in range(E // P)]
+        note_rows = [sb.tile([P, U], F32, name="note%d" % t) for t in range(PACK)]
+        val_rows = [sb.tile([P, T], F32, name="val%d" % b, tag="val%d" % b, align_bytes=ALIGN) for b in range(E // P)]
         lam_t = sb.tile([P, 1], F32, name="lam_t")
-        os_t = sb.tile([P, PACK], F32, name="os_t")
-        tgt = sb.tile([P, E], F32, name="tgt")
+        factor_t = sb.tile([P, PACK], F32, name="factor_t")
+        target_t = sb.tile([P, E], F32, name="target_t")
         ident = sb.tile([P, P], F32, name="ident")
 
-        nc.gpsimd.memset(ks[:].bitcast(I32), 0)
-        notes_v = notes.rearrange("(p j) u -> p j u", j=PACK)
+        nc.gpsimd.memset(key_scales[:].bitcast(I32), 0)
+        notes_by_place = notes.rearrange("(p t) u -> p t u", t=PACK)
         nc.sync.dma_start(offs_t[:], offs)
+        nc.sync.dma_start(offs2_t[:], offs2)
         for h in range(2):
             cols = slice(h * T // 4, (h + 1) * T // 4)
-            nc.sync.dma_start(out=kw[:].bitcast(I32)[:, cols], in_=keys_words[0].bitcast(I32)[:, cols])
-        nc.sync.dma_start(offs2_t[:], offs2)
+            nc.sync.dma_start(out=key_words[:].bitcast(I32)[:, cols], in_=keys_words[0].bitcast(I32)[:, cols])
         nc.scalar.dma_start(out=lam_t[:], in_=lam)
-        nc.scalar.dma_start(out=os_t[:], in_=factor.rearrange("o (p t) -> (o p) t", t=PACK))
-        nc.sync.dma_start(out=planes[0][:], in_=notes_v[:, 0, :])
-        nc.sync.dma_start(out=q_raw[:], in_=query.rearrange("(p j) w -> p j w", j=PACK))
-        for g in range(4):
-            nc.sync.dma_start(out=ks[32 * g : 32 * g + 4, :].bitcast(I32), in_=keys_scales[0, 4 * g : 4 * g + 4, :].bitcast(I32))
+        nc.scalar.dma_start(out=factor_t[:], in_=factor.rearrange("o (p t) -> (o p) t", t=PACK))
+        nc.sync.dma_start(out=note_rows[0][:], in_=notes_by_place[:, 0, :])
+        nc.sync.dma_start(out=q_raw[:], in_=query.rearrange("(p t) q -> p t q", t=PACK))
+        for g in range(QUADRANTS):
+            nc.sync.dma_start(out=key_scales[32 * g : 32 * g + 4, :].bitcast(I32), in_=keys_scales[0, 4 * g : 4 * g + 4, :].bitcast(I32))
         for t in range(1, PACK):
-            nc.sync.dma_start(out=planes[t][:], in_=notes_v[:, t, :])
-        nc.sync.dma_start(out=q2_raw[:], in_=query2.rearrange("(p j) w -> p j w", j=PACK))
+            nc.sync.dma_start(out=note_rows[t][:], in_=notes_by_place[:, t, :])
+        nc.sync.dma_start(out=q2_raw[:], in_=query2.rearrange("(p t) q -> p t q", t=PACK))
         for b in range(E // P):
-            nc.sync.dma_start(out=vblocks[b][:], in_=vals[b * P : (b + 1) * P, :])
-        nc.sync.dma_start(out=tgt[:], in_=target)
+            nc.sync.dma_start(out=val_rows[b][:], in_=vals[b * P : (b + 1) * P, :])
+        nc.sync.dma_start(out=target_t[:], in_=target)
         make_identity(nc, ident[:])
-        floor = sb.tile([P, 1], F32, name="floor", tag="floor", align_bytes=64)
-        nc.gpsimd.memset(floor[:], TINY)
+        floor = sb.tile([P, 1], F32, name="floor", tag="floor", align_bytes=ALIGN)
+        nc.gpsimd.memset(floor[:], SUM_FLOOR)
 
-        kwg = sb.tile([P, I], U16, name="kwg", align_bytes=64)
-        ksg = sb.tile([P, I], U8, name="ksg", align_bytes=64)
-        nc.vector.tensor_copy(kwg[:], kw[:].indirect(offs_t[:]))
-        ng = sb.tile([P, PACK, I], BF16, name="ng", tag="ng", align_bytes=64)
-        nc.vector.tensor_copy(ng[:, 0, :], planes[0][:].indirect(offs2_t[:]))
-        nc.vector.tensor_copy(ksg[:], ks[:].indirect(offs_t[:]))
+        keys_picked = sb.tile([P, I], U16, name="keys_picked", align_bytes=ALIGN)
+        key_scales_picked = sb.tile([P, I], U8, name="key_scales_picked", align_bytes=ALIGN)
+        nc.vector.tensor_copy(keys_picked[:], key_words[:].indirect(offs_t[:]))
+        notes_picked = sb.tile([P, PACK, I], BF16, name="notes_picked", tag="notes_picked", align_bytes=ALIGN)
+        nc.vector.tensor_copy(notes_picked[:, 0, :], note_rows[0][:].indirect(offs2_t[:]))
+        nc.vector.tensor_copy(key_scales_picked[:], key_scales[:].indirect(offs_t[:]))
 
-        def quantise_queries(raw, name, copy):
-            woven = sb.tile([P, Q, PACK], BF16, name=name + "_woven", align_bytes=64)
-            codes = sb.tile([P, Q], U32, name=name + "_codes", align_bytes=64)
-            scales = sb.tile([P, Q], U8, name=name + "_scales", align_bytes=64)
-            copy(out=woven[:].rearrange("p (c i) t -> p c t i", i=4), in_=raw[:].rearrange("p t (c i) -> p c t i", i=4))
-            nc.vector.quantize_mx(out=codes[:].bitcast(FP8X4), scales=scales[:], in_=woven[:].rearrange("p w j -> p (w j)"))
+        def quantise_queries(raw, name):
+            woven = sb.tile([P, Q, PACK], BF16, name=name + "_woven", align_bytes=ALIGN)
+            codes = sb.tile([P, Q], U32, name=name + "_codes", align_bytes=ALIGN)
+            scales = sb.tile([P, Q], U8, name=name + "_scales", align_bytes=ALIGN)
+            weave(nc.scalar.copy, woven[:], raw[:])
+            quantise(codes[:], scales[:], woven[:])
             return codes, scales
 
-        qc, qs = quantise_queries(q_raw, "q", nc.scalar.copy)
+        q_codes, q_scales = quantise_queries(q_raw, "q")
         a_ps = psum.tile([P, I], F32, name="a_ps", tag="a")
-        nc.tensor.matmul_mx(out=a_ps[:], lhsT=qc[:].bitcast(FP8X4), lhsT_scale=qs[:], rhs=kwg[:].bitcast(FP4X4), rhs_scale=ksg[:], start=True, stop=True)
+        nc.tensor.matmul_mx(out=a_ps[:], lhsT=q_codes[:].bitcast(FP8X4), lhsT_scale=q_scales[:], rhs=keys_picked[:].bitcast(FP4X4), rhs_scale=key_scales_picked[:], start=True, stop=True)
 
-        nb = sb.tile([P, U], BF16, name="nb", tag="nb")
-        nc.scalar.activation(out=nb[:], in_=planes[1][:], func=ACT.Copy)
-        nc.scalar.activation(out=ng[:, 1, :], in_=nb[:].indirect(offs2_t[:]), func=ACT.Copy)
+        note1_bf16 = sb.tile([P, U], BF16, name="note1_bf16")
+        nc.scalar.activation(out=note1_bf16[:], in_=note_rows[1][:], func=ACT.Copy)
+        nc.scalar.activation(out=notes_picked[:, 1, :], in_=note1_bf16[:].indirect(offs2_t[:]), func=ACT.Copy)
         for t in range(2, PACK):
-            nc.vector.tensor_copy(ng[:, t, :], planes[t][:].indirect(offs2_t[:]))
-        HI = I // 2
-        nw = [sb.tile([P, HI, PACK], BF16, name="nw%d" % h, tag="nw%d" % h, align_bytes=64) for h in range(2)]
-        for h, copy in enumerate((nc.vector.tensor_copy, nc.scalar.copy)):
-            copy(out=nw[h][:].rearrange("p (c i) t -> p c t i", i=4), in_=ng[:, :, h * HI : (h + 1) * HI].rearrange("p t (c i) -> p c t i", i=4))
-            if h == 0:
-                q2c, q2s = quantise_queries(q2_raw, "q2", nc.scalar.copy)
+            nc.vector.tensor_copy(notes_picked[:, t, :], note_rows[t][:].indirect(offs2_t[:]))
+        notes_woven = [
+            sb.tile([P, HALF_SLOTS, PACK], BF16, name="notes_woven0", align_bytes=ALIGN),
+            sb.tile([P, HALF_SLOTS, PACK], BF16, name="notes_woven1", tag="q2_raw", align_bytes=ALIGN),
+        ]
+        weave(nc.vector.tensor_copy, notes_woven[0][:], notes_picked[:, :, :HALF_SLOTS])
+        q2_codes, q2_scales = quantise_queries(q2_raw, "q2")
+        weave(nc.scalar.copy, notes_woven[1][:], notes_picked[:, :, HALF_SLOTS:])
         b_ps = []
         for h in range(2):
-            ncodes = sb.tile([P, HI], U32, name="ncodes%d" % h, align_bytes=64)
-            nscales = sb.tile([P, HI], U8, name="nscales%d" % h, align_bytes=64)
-            nc.vector.quantize_mx(out=ncodes[:].bitcast(FP8X4), scales=nscales[:], in_=nw[h][:].rearrange("p w j -> p (w j)"))
-            b_ps.append(psum.tile([P, HI], F32, name="b_ps%d" % h, tag="b%d" % h))
-            nc.tensor.matmul_mx(out=b_ps[h][:], lhsT=q2c[:].bitcast(FP8X4), lhsT_scale=q2s[:], rhs=ncodes[:].bitcast(FP8X4), rhs_scale=nscales[:], start=True, stop=True)
+            note_codes = sb.tile([P, HALF_SLOTS], U32, name="note_codes%d" % h, align_bytes=ALIGN)
+            note_scales = sb.tile([P, HALF_SLOTS], U8, name="note_scales%d" % h, align_bytes=ALIGN)
+            quantise(note_codes[:], note_scales[:], notes_woven[h][:])
+            b_ps.append(psum.tile([P, HALF_SLOTS], F32, name="b_ps%d" % h))
+            nc.tensor.matmul_mx(out=b_ps[h][:], lhsT=q2_codes[:].bitcast(FP8X4), lhsT_scale=q2_scales[:], rhs=note_codes[:].bitcast(FP8X4), rhs_scale=note_scales[:], start=True, stop=True)
 
-        def value_block(b, gathered_tag, vt_ps):
-            vg = sb.tile([P, I], BF16, name="vg%d" % b, tag=gathered_tag, align_bytes=64)
-            nc.vector.tensor_copy(vg[:], vblocks[b][:].indirect(offs_t[:]))
-            words = vg[:].bitcast(F32)
+        def gather_and_turn_values(b, tag, turned):
+            picked = sb.tile([P, I], BF16, name="vals_picked%d" % b, tag=tag, align_bytes=ALIGN)
+            nc.vector.tensor_copy(picked[:], val_rows[b][:].indirect(offs_t[:]))
+            pairs = picked[:].bitcast(F32)
             for u in range(2):
-                nc.tensor.transpose(vt_ps[:, u, :], words[:, u : I // 2 : 2], ident[:])
+                nc.tensor.transpose(turned[:, u, :], pairs[:, u : I // 2 : 2], ident[:])
 
-        def weave_values(vw, vt_ps):
-            nc.scalar.copy(out=vw.bitcast(F32), in_=vt_ps.rearrange("p u e -> p e u"))
+        def weave_values(woven, turned):
+            nc.scalar.copy(out=woven.bitcast(F32), in_=turned.rearrange("p u e -> p e u"))
 
-        def quantise(codes, scales, woven):
-            nc.vector.quantize_mx(out=codes.bitcast(FP8X4), scales=scales, in_=woven.rearrange("p e j -> p (e j)"))
+        lam_less_a = sb.tile([P, PACK, P], F32, name="lam_less_a", tag="notes_picked", align_bytes=ALIGN)
+        tanh_b = sb.tile([P, PACK, P], F32, name="tanh_b")
+        slot_halves = [slice(h * P // 2, (h + 1) * P // 2) for h in range(2)]
+        nc.scalar.activation(out=lam_less_a[:], in_=a_ps[:].rearrange("q (p t) -> q t p", t=PACK), func=ACT.Identity, bias=lam_t[:], scale=-1.0)
+        for h in range(2):
+            nc.scalar.activation(out=tanh_b[:, :, slot_halves[h]], in_=b_ps[h][:].rearrange("q (p t) -> q t p", t=PACK), func=ACT.Tanh, scale=0.5)
+        turned0 = psum.tile([P, 2, P], F32, name="turned0")
+        gather_and_turn_values(0, "q2_raw", turned0[:])
+        twice_neg = sb.tile([P, I], F32, name="twice_neg", tag="val0", align_bytes=ALIGN)
+        twice_neg_dealt = twice_neg[:].rearrange("q (t p) -> q t p", t=PACK)
+        for cols in slot_halves:
+            nc.vector.scalar_tensor_tensor(out=twice_neg_dealt[:, :, cols], in0=tanh_b[:, :, cols], scalar=1.0, in1=lam_less_a[:, :, cols], op0=ALU.add, op1=ALU.mult)
 
-        am = sb.tile([P, PACK, P], F32, name="am", tag="ng", align_bytes=64)
-        th = sb.tile([P, PACK, P], F32, name="th")
-        nc.scalar.activation(out=am[:], in_=a_ps[:].rearrange("q (p t) -> q t p", t=PACK), func=ACT.Identity, bias=lam_t[:], scale=-1.0)
+        neg = sb.tile([P, I], F32, name="neg", tag="neg", align_bytes=ALIGN)
+        neg_min = sb.tile([P, 1], F32, name="neg_min")
+        nc.vector.tensor_scalar(out=neg[:], in0=twice_neg[:], scalar1=0.5, scalar2=None, op0=ALU.mult, op1=ALU.min, accum_out=neg_min[:])
+        p_exp = sb.tile([P, I], F32, name="p_exp", tag="p_exp", align_bytes=ALIGN)
+        row_sum = sb.tile([P, 1], F32, name="row_sum", tag="row_sum", align_bytes=ALIGN)
+        nc.scalar.activation(out=p_exp[:], in_=neg[:], func=ACT.Exp, bias=neg_min[:], scale=-1.0, accum_out=row_sum[:])
+        turned1 = psum.tile([P, 2, P], F32, name="turned1", tag="a")
+        gather_and_turn_values(1, "val0", turned1[:])
+        vals_woven0 = sb.tile([P, P, PACK], BF16, name="vals_woven0", tag="neg", align_bytes=ALIGN)
+        weave_values(vals_woven0[:], turned0[:])
+        row_inv = sb.tile([P, 1], F32, name="row_inv", tag="val1", align_bytes=ALIGN)
+        nc.vector.reciprocal(row_inv[:], row_sum[:])
+        shares = sb.tile([P, I], F32, name="shares")
         for h in range(2):
-            nc.scalar.activation(out=th[:, :, h * P // 2 : (h + 1) * P // 2], in_=b_ps[h][:].rearrange("q (p t) -> q t p", t=PACK), func=ACT.Tanh, scale=0.5)
-        vt0 = psum.tile([P, 2, P], F32, name="vt0", tag="vt")
-        value_block(0, "nw1", vt0[:])
-        z = sb.tile([P, I], F32, name="z", tag="val0", align_bytes=64)
-        z_v = z[:].rearrange("q (t p) -> q t p", t=PACK)
-        for h in range(2):
-            cols = slice(h * P // 2, (h + 1) * P // 2)
-            nc.vector.scalar_tensor_tensor(out=z_v[:, :, cols], in0=th[:, :, cols], scalar=1.0, in1=am[:, :, cols], op0=ALU.add, op1=ALU.mult)
-        zh = sb.tile([P, I], F32, name="zh", tag="zh", align_bytes=64)
-        zmin = sb.tile([P, 1], F32, name="zmin")
-        nc.vector.tensor_scalar(out=zh[:], in0=z[:], scalar1=0.5, scalar2=None, op0=ALU.mult, op1=ALU.min, accum_out=zmin[:])
-        pexp = sb.tile([P, I], F32, name="pexp", tag="pexp", align_bytes=64)
-        psumr = sb.tile([P, 1], F32, name="psumr", tag="psumr", align_bytes=64)
-        nc.scalar.activation(out=pexp[:], in_=zh[:], func=ACT.Exp, bias=zmin[:], scale=-1.0, accum_out=psumr[:])
-        vt1 = psum.tile([P, 2, P], F32, name="vt1", tag="a")
-        value_block(1, "val0", vt1[:])
-        vw0 = sb.tile([P, P, PACK], BF16, name="vw0", tag="zh", align_bytes=64)
-        weave_values(vw0[:], vt0[:])
-        rinv = sb.tile([P, 1], F32, name="rinv", tag="val1", align_bytes=64)
-        nc.vector.reciprocal(rinv[:], psumr[:])
-        r = sb.tile([P, I], F32, name="r")
-        for h in range(2):
-            cols = slice(h * HI, (h + 1) * HI)
-            nc.scalar.activation(out=r[:, cols], in_=pexp[:, cols], func=ACT.Copy, scale=rinv[:])
-        vw1 = sb.tile([P, P, PACK], BF16, name="vw1", tag="pexp", align_bytes=64)
-        weave_values(vw1[:], vt1[:])
-        warm = sb.tile([P, 1], F32, name="warm")
-        nc.scalar.activation(out=warm[:], in_=r[:, I - 1 :], func=ACT.Abs_reciprocal_sqrt, bias=floor[:])
-        rt_ps = psum.tile([P, PACK, Q], F32, name="rt_ps")
+            cols = slice(h * 2 * P, (h + 1) * 2 * P)
+            nc.scalar.activation(out=shares[:, cols], in_=p_exp[:, cols], func=ACT.Copy, scale=row_inv[:])
+        vals_woven1 = sb.tile([P, P, PACK], BF16, name="vals_woven1", tag="p_exp", align_bytes=ALIGN)
+        weave_values(vals_woven1[:], turned1[:])
+        shares_t = psum.tile([P, PACK, Q], F32, name="shares_t")
         for t in range(PACK):
-            nc.tensor.transpose(rt_ps[:, t, :], r[:, t * P : (t + 1) * P], ident[:])
-        vt23 = psum.tile([P, 2, 2, P], F32, name="vt23", tag="a")
-        value_block(2, "psumr", vt23[:, 0])
-        value_block(3, "vg3", vt23[:, 1])
-        rg = sb.tile([P, K, PACK], F32, name="rg", tag="val3", align_bytes=64)
-        vscales = [sb.tile([P, 2 * P], U8, name="vscales%d" % h, align_bytes=64) for h in range(2)]
-        rto = sb.tile([P, K, GROUP, PACK], F32, name="rto")
-        rq = sb.tile([P, K, PACK], F32, name="rq")
-        ww = sb.tile([P, Q, PACK], BF16, name="ww", align_bytes=64)
-        ww_v = ww[:].rearrange("p (k j) t -> p k j t", j=GROUP)
-        halves = [slice(h * K // 2, (h + 1) * K // 2) for h in range(2)]
-        for ks_ in halves:
-            nc.vector.tensor_reduce(out=rg[:, ks_], in_=rt_ps[:].rearrange("p t (k j) -> p k t j", j=GROUP)[:, ks_], axis=AX.X, op=ALU.add)
-            nc.scalar.activation(out=rq[:, ks_], in_=rg[:, ks_], func=ACT.Abs_reciprocal_sqrt, bias=floor[:])
-        for ks_ in halves:
-            nc.vector.tensor_tensor(out=rto[:, ks_], in0=rt_ps[:].rearrange("p t (k j) -> p k j t", j=GROUP)[:, ks_], in1=os_t[:].unsqueeze(1).unsqueeze(1).broadcast_to([P, K // 2, GROUP, PACK]), op=ALU.mult)
-        vw23 = sb.tile([P, 2, P, PACK], BF16, name="vw23", tag="floor", align_bytes=64)
-        nc.scalar.copy(out=vw23[:].bitcast(F32), in_=vt23[:].rearrange("p b u e -> p b e u"))
-        for ks_ in halves:
-            nc.vector.tensor_tensor(out=ww_v[:, ks_], in0=rto[:, ks_], in1=rq[:, ks_].unsqueeze(2).broadcast_to([P, K // 2, GROUP, PACK]), op=ALU.mult)
-        vcodes = [sb.tile([P, 2 * P], U32, name="vcodes0", tag="val3", align_bytes=64), sb.tile([P, 2 * P], U32, name="vcodes1", align_bytes=64)]
-        quantise(vcodes[0][:, :P], vscales[0][:, :P], vw0[:])
-        quantise(vcodes[0][:, P:], vscales[0][:, P:], vw1[:])
-        wcodes = sb.tile([P, Q], U32, name="wcodes", align_bytes=64)
-        wscales = sb.tile([P, Q], U8, name="wscales", align_bytes=64)
-        quantise(wcodes[:], wscales[:], ww[:])
-        quantise(vcodes[1][:], vscales[1][:], vw23[:].rearrange("p b e j -> p (b e) j"))
+            nc.tensor.transpose(shares_t[:, t, :], shares[:, t * P : (t + 1) * P], ident[:])
+        turned23 = psum.tile([P, 2, 2, P], F32, name="turned23", tag="a")
+        gather_and_turn_values(2, "row_sum", turned23[:, 0])
+        gather_and_turn_values(3, "vals_picked3", turned23[:, 1])
 
-        H = E // 2
-        rs_a = sb.tile([P, H + 1], F32, name="rs_a")
-        rs_b = sb.tile([P, H], F32, name="rs_b")
-        nc.gpsimd.memset(rs_a[:, H : H + 1], 16.0)
-        for h, rs in enumerate((rs_a, rs_b)):
-            o_ps = psum.tile([P, H], F32, name="o_ps%d" % h)
-            cols = slice(h * H, (h + 1) * H)
-            nc.tensor.matmul_mx(out=o_ps[:], lhsT=wcodes[:].bitcast(FP8X4), lhsT_scale=wscales[:], rhs=vcodes[h][:, :].bitcast(FP8X4), rhs_scale=vscales[h][:], start=True, stop=True)
-            nc.vector.tensor_tensor(out=rs[:, :H], in0=tgt[:, cols], in1=o_ps[:], op=ALU.subtract)
-        sq_a = sb.tile([P, H + 1], F32, name="sq_a")
-        sq_b = sb.tile([P, H], F32, name="sq_b")
-        ssq_a = sb.tile([P, 1], F32, name="ssq_a")
-        ssq_b = sb.tile([P, 1], F32, name="ssq_b")
-        nc.scalar.activation(out=sq_a[:], in_=rs_a[:], func=ACT.Square, accum_out=ssq_a[:])
-        nc.vector.scalar_tensor_tensor(out=sq_b[:], in0=rs_b[:], scalar=1.0 / E, in1=rs_b[:], op0=ALU.mult, op1=ALU.mult, accum_out=ssq_b[:])
-        kinv = sb.tile([P, 1], F32, name="kinv")
-        nc.scalar.activation(out=kinv[:], in_=ssq_a[:], func=ACT.Abs_reciprocal_sqrt, scale=1.0 / E, bias=ssq_b[:])
-        y_a = sb.tile([P, H], F32, name="y_a")
-        y_b = sb.tile([P, H], F32, name="y_b")
-        nc.vector.tensor_scalar(out=y_a[:], in0=rs_a[:, :H], scalar1=kinv[:], scalar2=None, op0=ALU.mult)
-        nc.sync.dma_start(out=out[:, :H], in_=y_a[:])
-        nc.scalar.activation(out=y_b[:], in_=rs_b[:], func=ACT.Copy, scale=kinv[:])
-        nc.scalar.dma_start(out=out[:, H:], in_=y_b[:])
+        group_sum = sb.tile([P, K, PACK], F32, name="group_sum", tag="val3", align_bytes=ALIGN)
+        val_scales = [sb.tile([P, HALF_FEATURES], U8, name="val_scales%d" % h, align_bytes=ALIGN) for h in range(2)]
+        scaled_shares = sb.tile([P, K, GROUP, PACK], F32, name="scaled_shares")
+        inv_root = sb.tile([P, K, PACK], F32, name="inv_root")
+        w_woven = sb.tile([P, Q, PACK], BF16, name="w_woven", align_bytes=ALIGN)
+        w_by_group = w_woven[:].rearrange("p (k j) t -> p k j t", j=GROUP)
+        group_halves = [slice(h * K // 2, (h + 1) * K // 2) for h in range(2)]
+        half_shape = [P, K // 2, GROUP, PACK]
+        for groups in group_halves:
+            nc.vector.tensor_reduce(out=group_sum[:, groups], in_=shares_t[:].rearrange("p t (k j) -> p k t j", j=GROUP)[:, groups], axis=AX.X, op=ALU.add)
+            nc.scalar.activation(out=inv_root[:, groups], in_=group_sum[:, groups], func=ACT.Abs_reciprocal_sqrt, bias=floor[:])
+        for groups in group_halves:
+            nc.vector.tensor_tensor(
+                out=scaled_shares[:, groups],
+                in0=shares_t[:].rearrange("p t (k j) -> p k j t", j=GROUP)[:, groups],
+                in1=factor_t[:].unsqueeze(1).unsqueeze(1).broadcast_to(half_shape),
+                op=ALU.mult,
+            )
+        vals_woven23 = sb.tile([P, 2, P, PACK], BF16, name="vals_woven23", tag="floor", align_bytes=ALIGN)
+        nc.scalar.copy(out=vals_woven23[:].bitcast(F32), in_=turned23[:].rearrange("p b u e -> p b e u"))
+        for groups in group_halves:
+            nc.vector.tensor_tensor(out=w_by_group[:, groups], in0=scaled_shares[:, groups], in1=inv_root[:, groups].unsqueeze(2).broadcast_to(half_shape), op=ALU.mult)
+        val_codes = [
+            sb.tile([P, HALF_FEATURES], U32, name="val_codes0", tag="val3", align_bytes=ALIGN),
+            sb.tile([P, HALF_FEATURES], U32, name="val_codes1", align_bytes=ALIGN),
+        ]
+        quantise(val_codes[0][:, :P], val_scales[0][:, :P], vals_woven0[:])
+        quantise(val_codes[0][:, P:], val_scales[0][:, P:], vals_woven1[:])
+        w_codes = sb.tile([P, Q], U32, name="w_codes", align_bytes=ALIGN)
+        w_scales = sb.tile([P, Q], U8, name="w_scales", align_bytes=ALIGN)
+        quantise(w_codes[:], w_scales[:], w_woven[:])
+        quantise(val_codes[1][:], val_scales[1][:], vals_woven23[:].rearrange("p b e t -> p (b e) t"))
+
+        rest_a = sb.tile([P, HALF_FEATURES + 1], F32, name="rest_a")
+        rest_b = sb.tile([P, HALF_FEATURES], F32, name="rest_b")
+        nc.gpsimd.memset(rest_a[:, HALF_FEATURES:], PAD_VALUE)
+        for h, rest in enumerate((rest_a, rest_b)):
+            o_ps = psum.tile([P, HALF_FEATURES], F32, name="o_ps%d" % h)
+            cols = slice(h * HALF_FEATURES, (h + 1) * HALF_FEATURES)
+            nc.tensor.matmul_mx(out=o_ps[:], lhsT=w_codes[:].bitcast(FP8X4), lhsT_scale=w_scales[:], rhs=val_codes[h][:].bitcast(FP8X4), rhs_scale=val_scales[h][:], start=True, stop=True)
+            nc.vector.tensor_tensor(out=rest[:, :HALF_FEATURES], in0=target_t[:, cols], in1=o_ps[:], op=ALU.subtract)
+        squares_a = sb.tile([P, HALF_FEATURES + 1], F32, name="squares_a")
+        squares_b = sb.tile([P, HALF_FEATURES], F32, name="squares_b")
+        sum_a = sb.tile([P, 1], F32, name="sum_a")
+        mean_b = sb.tile([P, 1], F32, name="mean_b")
+        nc.scalar.activation(out=squares_a[:], in_=rest_a[:], func=ACT.Square, accum_out=sum_a[:])
+        nc.vector.scalar_tensor_tensor(out=squares_b[:], in0=rest_b[:], scalar=1.0 / E, in1=rest_b[:], op0=ALU.mult, op1=ALU.mult, accum_out=mean_b[:])
+        inv_norm = sb.tile([P, 1], F32, name="inv_norm")
+        nc.scalar.activation(out=inv_norm[:], in_=sum_a[:], func=ACT.Abs_reciprocal_sqrt, scale=1.0 / E, bias=mean_b[:])
+        y_a = sb.tile([P, HALF_FEATURES], F32, name="y_a")
+        y_b = sb.tile([P, HALF_FEATURES], F32, name="y_b")
+        nc.vector.tensor_scalar(out=y_a[:], in0=rest_a[:, :HALF_FEATURES], scalar1=inv_norm[:], scalar2=None, op0=ALU.mult)
+        nc.sync.dma_start(out=out[:, :HALF_FEATURES], in_=y_a[:])
+        nc.scalar.activation(out=y_b[:], in_=rest_b[:], func=ACT.Copy, scale=inv_norm[:])
+        nc.scalar.dma_start(out=out[:, HALF_FEATURES:], in_=y_b[:])

from contextlib import ExitStack

import concourse.mybir as mybir
from concourse.masks import make_identity

D, T, I, Q, E, U, K = 512, 2048, 512, 128, 512, 1024, 16
FLOPS = 2 * Q * I * D * 2 + 2 * Q * E * I

F32 = mybir.dt.float32
BF16 = mybir.dt.bfloat16
I32 = mybir.dt.int32
U32 = mybir.dt.uint32
U16 = mybir.dt.uint16
U8 = mybir.dt.uint8
FP8X4 = mybir.dt.float8_e4m3fn_x4
FP4X4 = mybir.dt.float4_e2m1fn_x4
ACT = mybir.ActivationFunctionType
ALU = mybir.AluOpType
AX = mybir.AxisListType

P = 128
PACK = 4
QUADRANTS = 4
LIST_COLUMNS = I // 16
GROUP = Q // K
HALF_SLOTS = I // 2
HALF_FEATURES = E // 2
RUN = 4
ALIGN = 64
SUM_FLOOR = 2.0**-100
PAD_VALUE = 16.0


def tile_attend_tilted_balanced_remainder_kernel(tc, query, query2, keys_words, keys_scales, notes, lam, factor, vals, target, offs, offs2, out):
    nc = tc.nc
    with ExitStack() as ctx:
        lists = ctx.enter_context(tc.tile_pool(name="lists", bufs=1))
        sb = ctx.enter_context(tc.tile_pool(name="sb", bufs=1))
        psum = ctx.enter_context(tc.psum_pool(name="psum", bufs=1))

        def quantise(codes, scales, woven):
            nc.vector.quantize_mx(out=codes.bitcast(FP8X4), scales=scales, in_=woven.rearrange("p c t -> p (c t)"))

        def weave(copy, woven, by_place):
            copy(out=woven.rearrange("p (c i) t -> p c t i", i=RUN), in_=by_place.rearrange("p t (c i) -> p c t i", i=RUN))

        offs_t = lists.tile([P, LIST_COLUMNS], U16, name="offs_t")
        offs2_t = lists.tile([P, LIST_COLUMNS], U16, name="offs2_t")
        key_words = sb.tile([P, T], U16, name="key_words", align_bytes=ALIGN)
        key_scales = sb.tile([P, T], U8, name="key_scales", align_bytes=ALIGN)
        q2_raw = sb.tile([P, PACK, Q], F32, name="q2_raw", tag="q2_raw", align_bytes=ALIGN)
        q_raw = sb.tile([P, PACK, Q], F32, name="q_raw")
        note_rows = [sb.tile([P, U], F32, name="note%d" % t) for t in range(PACK)]
        val_rows = [sb.tile([P, T], F32, name="val%d" % b, tag="val%d" % b, align_bytes=ALIGN) for b in range(E // P)]
        lam_t = sb.tile([P, 1], F32, name="lam_t")
        factor_t = sb.tile([P, PACK], F32, name="factor_t")
        target_t = sb.tile([P, E], F32, name="target_t")
        ident = sb.tile([P, P], F32, name="ident")

        nc.gpsimd.memset(key_scales[:].bitcast(I32), 0)
        notes_by_place = notes.rearrange("(p t) u -> p t u", t=PACK)
        nc.sync.dma_start(offs_t[:], offs)
        nc.sync.dma_start(offs2_t[:], offs2)
        for h in range(2):
            cols = slice(h * T // 4, (h + 1) * T // 4)
            nc.sync.dma_start(out=key_words[:].bitcast(I32)[:, cols], in_=keys_words[0].bitcast(I32)[:, cols])
        nc.scalar.dma_start(out=lam_t[:], in_=lam)
        nc.scalar.dma_start(out=factor_t[:], in_=factor.rearrange("o (p t) -> (o p) t", t=PACK))
        nc.sync.dma_start(out=note_rows[0][:], in_=notes_by_place[:, 0, :])
        nc.sync.dma_start(out=q_raw[:], in_=query.rearrange("(p t) q -> p t q", t=PACK))
        for g in range(QUADRANTS):
            nc.sync.dma_start(out=key_scales[32 * g : 32 * g + 4, :].bitcast(I32), in_=keys_scales[0, 4 * g : 4 * g + 4, :].bitcast(I32))
        for t in range(1, PACK):
            nc.sync.dma_start(out=note_rows[t][:], in_=notes_by_place[:, t, :])
        nc.sync.dma_start(out=q2_raw[:], in_=query2.rearrange("(p t) q -> p t q", t=PACK))
        for b in range(E // P):
            nc.sync.dma_start(out=val_rows[b][:], in_=vals[b * P : (b + 1) * P, :])
        nc.sync.dma_start(out=target_t[:], in_=target)
        make_identity(nc, ident[:])
        floor = sb.tile([P, 1], F32, name="floor", tag="floor", align_bytes=ALIGN)
        nc.gpsimd.memset(floor[:], SUM_FLOOR)

        keys_picked = sb.tile([P, I], U16, name="keys_picked", align_bytes=ALIGN)
        key_scales_picked = sb.tile([P, I], U8, name="key_scales_picked", align_bytes=ALIGN)
        nc.vector.tensor_copy(keys_picked[:], key_words[:].indirect(offs_t[:]))
        notes_picked = sb.tile([P, PACK, I], BF16, name="notes_picked", tag="notes_picked", align_bytes=ALIGN)
        nc.vector.tensor_copy(notes_picked[:, 0, :], note_rows[0][:].indirect(offs2_t[:]))
        nc.vector.tensor_copy(key_scales_picked[:], key_scales[:].indirect(offs_t[:]))

        def quantise_queries(raw, name):
            woven = sb.tile([P, Q, PACK], BF16, name=name + "_woven", align_bytes=ALIGN)
            codes = sb.tile([P, Q], U32, name=name + "_codes", align_bytes=ALIGN)
            scales = sb.tile([P, Q], U8, name=name + "_scales", align_bytes=ALIGN)
            weave(nc.scalar.copy, woven[:], raw[:])
            quantise(codes[:], scales[:], woven[:])
            return codes, scales

        q_codes, q_scales = quantise_queries(q_raw, "q")
        a_ps = psum.tile([P, I], F32, name="a_ps", tag="a")
        nc.tensor.matmul_mx(out=a_ps[:], lhsT=q_codes[:].bitcast(FP8X4), lhsT_scale=q_scales[:], rhs=keys_picked[:].bitcast(FP4X4), rhs_scale=key_scales_picked[:], start=True, stop=True)

        note1_bf16 = sb.tile([P, U], BF16, name="note1_bf16")
        nc.scalar.activation(out=note1_bf16[:], in_=note_rows[1][:], func=ACT.Copy)
        nc.scalar.activation(out=notes_picked[:, 1, :], in_=note1_bf16[:].indirect(offs2_t[:]), func=ACT.Copy)
        for t in range(2, PACK):
            nc.vector.tensor_copy(notes_picked[:, t, :], note_rows[t][:].indirect(offs2_t[:]))
        notes_woven = [
            sb.tile([P, HALF_SLOTS, PACK], BF16, name="notes_woven0", align_bytes=ALIGN),
            sb.tile([P, HALF_SLOTS, PACK], BF16, name="notes_woven1", tag="q2_raw", align_bytes=ALIGN),
        ]
        weave(nc.vector.tensor_copy, notes_woven[0][:], notes_picked[:, :, :HALF_SLOTS])
        q2_codes, q2_scales = quantise_queries(q2_raw, "q2")
        weave(nc.scalar.copy, notes_woven[1][:], notes_picked[:, :, HALF_SLOTS:])
        b_ps = []
        for h in range(2):
            note_codes = sb.tile([P, HALF_SLOTS], U32, name="note_codes%d" % h, align_bytes=ALIGN)
            note_scales = sb.tile([P, HALF_SLOTS], U8, name="note_scales%d" % h, align_bytes=ALIGN)
            quantise(note_codes[:], note_scales[:], notes_woven[h][:])
            b_ps.append(psum.tile([P, HALF_SLOTS], F32, name="b_ps%d" % h))
            nc.tensor.matmul_mx(out=b_ps[h][:], lhsT=q2_codes[:].bitcast(FP8X4), lhsT_scale=q2_scales[:], rhs=note_codes[:].bitcast(FP8X4), rhs_scale=note_scales[:], start=True, stop=True)

        def gather_and_turn_values(b, tag, turned):
            picked = sb.tile([P, I], BF16, name="vals_picked%d" % b, tag=tag, align_bytes=ALIGN)
            nc.vector.tensor_copy(picked[:], val_rows[b][:].indirect(offs_t[:]))
            pairs = picked[:].bitcast(F32)
            for u in range(2):
                nc.tensor.transpose(turned[:, u, :], pairs[:, u : I // 2 : 2], ident[:])

        def weave_values(woven, turned):
            nc.scalar.copy(out=woven.bitcast(F32), in_=turned.rearrange("p u e -> p e u"))

        lam_less_a = sb.tile([P, PACK, P], F32, name="lam_less_a", tag="notes_picked", align_bytes=ALIGN)
        tanh_b = sb.tile([P, PACK, P], F32, name="tanh_b")
        slot_halves = [slice(h * P // 2, (h + 1) * P // 2) for h in range(2)]
        nc.scalar.activation(out=lam_less_a[:], in_=a_ps[:].rearrange("q (p t) -> q t p", t=PACK), func=ACT.Identity, bias=lam_t[:], scale=-1.0)
        for h in range(2):
            nc.scalar.activation(out=tanh_b[:, :, slot_halves[h]], in_=b_ps[h][:].rearrange("q (p t) -> q t p", t=PACK), func=ACT.Tanh, scale=0.5)
        turned0 = psum.tile([P, 2, P], F32, name="turned0")
        gather_and_turn_values(0, "q2_raw", turned0[:])
        twice_neg = sb.tile([P, I], F32, name="twice_neg", tag="val0", align_bytes=ALIGN)
        twice_neg_dealt = twice_neg[:].rearrange("q (t p) -> q t p", t=PACK)
        for cols in slot_halves:
            nc.vector.scalar_tensor_tensor(out=twice_neg_dealt[:, :, cols], in0=tanh_b[:, :, cols], scalar=1.0, in1=lam_less_a[:, :, cols], op0=ALU.add, op1=ALU.mult)

        neg = sb.tile([P, I], F32, name="neg", tag="neg", align_bytes=ALIGN)
        neg_min = sb.tile([P, 1], F32, name="neg_min")
        nc.vector.tensor_scalar(out=neg[:], in0=twice_neg[:], scalar1=0.5, scalar2=None, op0=ALU.mult, op1=ALU.min, accum_out=neg_min[:])
        p_exp = sb.tile([P, I], F32, name="p_exp", tag="p_exp", align_bytes=ALIGN)
        row_sum = sb.tile([P, 1], F32, name="row_sum", tag="row_sum", align_bytes=ALIGN)
        nc.scalar.activation(out=p_exp[:], in_=neg[:], func=ACT.Exp, bias=neg_min[:], scale=-1.0, accum_out=row_sum[:])
        turned1 = psum.tile([P, 2, P], F32, name="turned1", tag="a")
        gather_and_turn_values(1, "val0", turned1[:])
        vals_woven0 = sb.tile([P, P, PACK], BF16, name="vals_woven0", tag="neg", align_bytes=ALIGN)
        weave_values(vals_woven0[:], turned0[:])
        row_inv = sb.tile([P, 1], F32, name="row_inv", tag="val1", align_bytes=ALIGN)
        nc.vector.reciprocal(row_inv[:], row_sum[:])
        shares = sb.tile([P, I], F32, name="shares")
        for h in range(2):
            cols = slice(h * 2 * P, (h + 1) * 2 * P)
            nc.scalar.activation(out=shares[:, cols], in_=p_exp[:, cols], func=ACT.Copy, scale=row_inv[:])
        vals_woven1 = sb.tile([P, P, PACK], BF16, name="vals_woven1", tag="p_exp", align_bytes=ALIGN)
        weave_values(vals_woven1[:], turned1[:])
        shares_t = psum.tile([P, PACK, Q], F32, name="shares_t")
        for t in range(PACK):
            nc.tensor.transpose(shares_t[:, t, :], shares[:, t * P : (t + 1) * P], ident[:])
        turned23 = psum.tile([P, 2, 2, P], F32, name="turned23", tag="a")
        gather_and_turn_values(2, "row_sum", turned23[:, 0])
        gather_and_turn_values(3, "vals_picked3", turned23[:, 1])

        group_sum = sb.tile([P, K, PACK], F32, name="group_sum", tag="val3", align_bytes=ALIGN)
        val_scales = [sb.tile([P, HALF_FEATURES], U8, name="val_scales%d" % h, align_bytes=ALIGN) for h in range(2)]
        scaled_shares = sb.tile([P, K, GROUP, PACK], F32, name="scaled_shares")
        inv_root = sb.tile([P, K, PACK], F32, name="inv_root")
        w_woven = sb.tile([P, Q, PACK], BF16, name="w_woven", align_bytes=ALIGN)
        w_by_group = w_woven[:].rearrange("p (k j) t -> p k j t", j=GROUP)
        group_halves = [slice(h * K // 2, (h + 1) * K // 2) for h in range(2)]
        half_shape = [P, K // 2, GROUP, PACK]
        for groups in group_halves:
            nc.vector.tensor_reduce(out=group_sum[:, groups], in_=shares_t[:].rearrange("p t (k j) -> p k t j", j=GROUP)[:, groups], axis=AX.X, op=ALU.add)
            nc.scalar.activation(out=inv_root[:, groups], in_=group_sum[:, groups], func=ACT.Abs_reciprocal_sqrt, bias=floor[:])
        for groups in group_halves:
            nc.vector.tensor_tensor(
                out=scaled_shares[:, groups],
                in0=shares_t[:].rearrange("p t (k j) -> p k j t", j=GROUP)[:, groups],
                in1=factor_t[:].unsqueeze(1).unsqueeze(1).broadcast_to(half_shape),
                op=ALU.mult,
            )
        vals_woven23 = sb.tile([P, 2, P, PACK], BF16, name="vals_woven23", tag="floor", align_bytes=ALIGN)
        nc.scalar.copy(out=vals_woven23[:].bitcast(F32), in_=turned23[:].rearrange("p b u e -> p b e u"))
        for groups in group_halves:
            nc.vector.tensor_tensor(out=w_by_group[:, groups], in0=scaled_shares[:, groups], in1=inv_root[:, groups].unsqueeze(2).broadcast_to(half_shape), op=ALU.mult)
        val_codes = [
            sb.tile([P, HALF_FEATURES], U32, name="val_codes0", tag="val3", align_bytes=ALIGN),
            sb.tile([P, HALF_FEATURES], U32, name="val_codes1", align_bytes=ALIGN),
        ]
        quantise(val_codes[0][:, :P], val_scales[0][:, :P], vals_woven0[:])
        quantise(val_codes[0][:, P:], val_scales[0][:, P:], vals_woven1[:])
        w_codes = sb.tile([P, Q], U32, name="w_codes", align_bytes=ALIGN)
        w_scales = sb.tile([P, Q], U8, name="w_scales", align_bytes=ALIGN)
        quantise(w_codes[:], w_scales[:], w_woven[:])
        quantise(val_codes[1][:], val_scales[1][:], vals_woven23[:].rearrange("p b e t -> p (b e) t"))

        rest_a = sb.tile([P, HALF_FEATURES + 1], F32, name="rest_a")
        rest_b = sb.tile([P, HALF_FEATURES], F32, name="rest_b")
        nc.gpsimd.memset(rest_a[:, HALF_FEATURES:], PAD_VALUE)
        for h, rest in enumerate((rest_a, rest_b)):
            o_ps = psum.tile([P, HALF_FEATURES], F32, name="o_ps%d" % h)
            cols = slice(h * HALF_FEATURES, (h + 1) * HALF_FEATURES)
            nc.tensor.matmul_mx(out=o_ps[:], lhsT=w_codes[:].bitcast(FP8X4), lhsT_scale=w_scales[:], rhs=val_codes[h][:].bitcast(FP8X4), rhs_scale=val_scales[h][:], start=True, stop=True)
            nc.vector.tensor_tensor(out=rest[:, :HALF_FEATURES], in0=target_t[:, cols], in1=o_ps[:], op=ALU.subtract)
        squares_a = sb.tile([P, HALF_FEATURES + 1], F32, name="squares_a")
        squares_b = sb.tile([P, HALF_FEATURES], F32, name="squares_b")
        sum_a = sb.tile([P, 1], F32, name="sum_a")
        mean_b = sb.tile([P, 1], F32, name="mean_b")
        nc.scalar.activation(out=squares_a[:], in_=rest_a[:], func=ACT.Square, accum_out=sum_a[:])
        nc.vector.scalar_tensor_tensor(out=squares_b[:], in0=rest_b[:], scalar=1.0 / E, in1=rest_b[:], op0=ALU.mult, op1=ALU.mult, accum_out=mean_b[:])
        inv_norm = sb.tile([P, 1], F32, name="inv_norm")
        nc.scalar.activation(out=inv_norm[:], in_=sum_a[:], func=ACT.Abs_reciprocal_sqrt, scale=1.0 / E, bias=mean_b[:])
        y_a = sb.tile([P, HALF_FEATURES], F32, name="y_a")
        y_b = sb.tile([P, HALF_FEATURES], F32, name="y_b")
        nc.vector.tensor_scalar(out=y_a[:], in0=rest_a[:, :HALF_FEATURES], scalar1=inv_norm[:], scalar2=None, op0=ALU.mult)
        nc.sync.dma_start(out=out[:, :HALF_FEATURES], in_=y_a[:])
        nc.scalar.activation(out=y_b[:], in_=rest_b[:], func=ACT.Copy, scale=inv_norm[:])
        nc.scalar.dma_start(out=out[:, HALF_FEATURES:], in_=y_b[:])
